import numpy as np
import ml_dtypes


def mxq(x, axis, fmt="e4m3"):
    dtype, down = {"e4m3": (ml_dtypes.float8_e4m3fn, 7), "e5m2": (ml_dtypes.float8_e5m2, 14)}[fmt]
    v = np.moveaxis(np.asarray(x, np.float32).astype(ml_dtypes.bfloat16).astype(np.float64), axis, -1)
    blocks = v.reshape(v.shape[:-1] + (-1, 32))
    amax = np.abs(blocks).max(-1, keepdims=True)
    byte = np.maximum(np.where(amax > 0, np.frexp(amax)[1] - 1 + 127, 0) - down, 1)
    scale = np.exp2(byte - 127.0)
    codes = (blocks / scale).astype(np.float32).astype(dtype).astype(np.float64)
    return np.moveaxis((codes * scale).reshape(v.shape), -1, axis)


WIDE = False


def mx_kscale(k):
    if not WIDE:
        return np.ones(k)
    levels = np.array([10, -10, 5, -5, 0])
    if k % 512:
        return np.exp2(np.random.permutation(np.resize(levels, k // 32))).repeat(32)
    a = np.empty((k // 512, 16))
    for p in range(k // 512):
        a[p, :8] = np.random.permutation(np.resize(levels, 8))
        for g in range(8):
            far = levels[np.abs(levels - a[p, g]) >= 10]
            a[p, g + 8] = far[np.random.randint(len(far))]
    return np.exp2(a.ravel()).repeat(32)


def f64(x):
    return np.asarray(x).astype(np.float64)


def striped(idx):
    return np.tile(idx.reshape(-1, 16).T, (8, 1)).astype(np.uint16)


def unstriped(offs):
    return offs[:16].T.reshape(-1).astype(np.int64)


def pack_weight(w):
    k, n = w.shape
    w = f64(np.asarray(w, np.float32).astype(ml_dtypes.bfloat16)).reshape(k // 32, 32, n)
    amax = np.abs(w).max(1)
    byte = np.clip(np.where(amax > 0, np.frexp(amax)[1] - 1 + 127 - 7, 1), 1, 254)
    scaled = (w * np.exp2(127.0 - byte)[:, None, :]).reshape(k, n).astype(np.float32)
    words = np.ascontiguousarray(scaled.reshape(k // 512, 128, 4, n).transpose(0, 1, 3, 2)).astype(ml_dtypes.float8_e4m3fn).view(np.uint8)
    return words, np.ascontiguousarray(byte.astype(np.uint8).reshape(k // 512, 16, n))


def unpack_weight(words, scales):
    g, p, n, _ = words.shape
    vals = np.ascontiguousarray(words).view(ml_dtypes.float8_e4m3fn).astype(np.float64) * np.repeat(np.exp2(scales.astype(np.float64) - 127.0), 8, axis=1)[..., None]
    return vals.transpose(0, 1, 3, 2).reshape(g * 512, n)


K, T, N, U = 512, 1024, 256, 2048


def setup_inputs():
    n = np.random.standard_normal
    s = mx_kscale(K)[:, None]
    packed_xT = pack_weight(n((K, T)) * s)
    return {
        "x_words": packed_xT[0],
        "x_scales": packed_xT[1],
        "mem": n((N, U)).astype(np.float32),
        "w1": (n((K, N)) / np.sqrt(K) / s).astype(np.float32),
        "slot": striped(np.random.permutation(U)[:T]),
    }


def reference(x_words, x_scales, mem, w1, slot):
    xq = unpack_weight(x_words, x_scales)
    y = np.tanh(mxq(f64(w1), 0, "e4m3").T @ xq)
    out = f64(mem).copy()
    out[:, unstriped(slot)] = y
    return out

@@ -1,0 +1,69 @@
+from contextlib import ExitStack
+
+import concourse.mybir as mybir
+
+F32 = mybir.dt.float32
+BF16 = mybir.dt.bfloat16
+I32 = mybir.dt.int32
+U32 = mybir.dt.uint32
+U16 = mybir.dt.uint16
+U8 = mybir.dt.uint8
+FP8X4 = mybir.dt.float8_e4m3fn_x4
+TANH = mybir.ActivationFunctionType.Tanh
+
+K, T, N, U = 512, 1024, 256, 2048
+P = 128
+FLOPS = 2 * K * T * N
+
+
+def tile_picked_wkvput_tanh_l_kernel(tc, x_words, x_scales, mem, w1, slot, out):
+    nc = tc.nc
+    with ExitStack() as ctx:
+        keep = ctx.enter_context(tc.tile_pool(name="keep", bufs=1))
+        psum = ctx.enter_context(tc.psum_pool(name="psum", bufs=1))
+
+        chunks = [(0, 256), (256, 512), (512, 1024)]
+        offsets = keep.tile([P, T // 16], U16, name="offsets")
+        w_raw = keep.tile([P, 4, N], F32, name="w_raw")
+        w_bf = [keep.tile([P, P, 4], BF16, name="w_bf%d" % b, align_bytes=64) for b in range(2)]
+        w_codes = [keep.tile([P, P], U32, name="w_codes%d" % b, align_bytes=64) for b in range(2)]
+        w_sc = [keep.tile([P, P], U8, name="w_sc%d" % b, align_bytes=64) for b in range(2)]
+        x_codes = [keep.tile([P, b - a], U32, name="x_codes%d" % a, align_bytes=64) for a, b in chunks]
+        x_sc = keep.tile([P, T], U8, name="x_sc", align_bytes=64)
+        win = [keep.tile([P, U], F32, name="win%d" % b) for b in range(2)]
+        w_view = w1.rearrange("(p j) n -> p j n", j=4)
+        x_view = x_words[0].rearrange("p n t -> p (n t)").bitcast(I32)
+        s_view = x_scales[0].bitcast(I32)
+
+        for q in range(4):
+            nc.scalar.dma_start(out=x_sc[32 * q : 32 * q + 4, :].bitcast(I32), in_=s_view[4 * q : 4 * q + 4, :])
+        nc.sync.dma_start(out=w_raw[:], in_=w_view)
+        nc.sync.dma_start(out=x_codes[0][:].bitcast(I32), in_=x_view[:, 0:256])
+        nc.sync.dma_start(offsets[:], slot)
+        nc.sync.dma_start(out=win[0][:], in_=mem[0:P, :])
+        nc.sync.dma_start(out=x_codes[1][:].bitcast(I32), in_=x_view[:, 256:512])
+        nc.sync.dma_start(out=x_codes[2][:].bitcast(I32), in_=x_view[:, 512:1024])
+        nc.sync.dma_start(out=win[1][:], in_=mem[P : 2 * P, :])
+
+        def product(b, c):
+            lo, hi = chunks[c]
+            acc = psum.tile([P, hi - lo], F32, name="acc%d_%d" % (b, c))
+            nc.tensor.matmul_mx(out=acc[:], lhsT=w_codes[b][:].bitcast(FP8X4), lhsT_scale=w_sc[b][:],
+                                rhs=x_codes[c][:].bitcast(FP8X4), rhs_scale=x_sc[:, lo:hi], start=True, stop=True)
+            return acc
+
+        for b in range(2):
+            nc.vector.tensor_copy(out=w_bf[b][:], in_=w_raw[:, :, b * P : (b + 1) * P].rearrange("p j w -> p w j"))
+        for b in range(2):
+            nc.vector.quantize_mx(out=w_codes[b][:].bitcast(FP8X4), scales=w_sc[b][:], in_=w_bf[b][:].rearrange("p w j -> p (w j)"))
+        y0 = [keep.tile([P, b - a], F32, name="y0_%d" % a) for a, b in chunks]
+        y1 = keep.tile([P, T], F32, name="y1")
+        for c in range(3):
+            nc.scalar.activation(out=y0[c][:], in_=product(0, c)[:], func=TANH)
+        for c in range(3):
+            nc.scalar.activation(out=y1[:, chunks[c][0] : chunks[c][1]], in_=product(1, c)[:], func=TANH)
+        for c in range(3):
+            nc.vector.tensor_copy(win[0][:].indirect(offsets[:, chunks[c][0] // 16 : chunks[c][1] // 16]), y0[c][:])
+        nc.sync.dma_start(out=out[0:P, :], in_=win[0][:])
+        nc.vector.tensor_copy(win[1][:].indirect(offsets[:]), y1[:])
+        nc.sync.dma_start(out=out[P : 2 * P, :], in_=win[1][:])

@@ -24,7 +24,7 @@ def tile_picked_wkvput_tanh_l_kernel(tc, x_words, x_scales, mem, w1, slot, out):
 
         chunks = [(0, 256), (256, 512), (512, 1024)]
         offsets = keep.tile([P, T // 16], U16, name="offsets")
-        w_raw = keep.tile([P, 4, N], F32, name="w_raw")
+        w_raw = [keep.tile([P, 4, P], F32, name="w_raw%d" % b) for b in range(2)]
         w_bf = [keep.tile([P, P, 4], BF16, name="w_bf%d" % b, align_bytes=64) for b in range(2)]
         w_codes = [keep.tile([P, P], U32, name="w_codes%d" % b, align_bytes=64) for b in range(2)]
         w_sc = [keep.tile([P, P], U8, name="w_sc%d" % b, align_bytes=64) for b in range(2)]
@@ -35,35 +35,38 @@ def tile_picked_wkvput_tanh_l_kernel(tc, x_words, x_scales, mem, w1, slot, out):
         x_view = x_words[0].rearrange("p n t -> p (n t)").bitcast(I32)
         s_view = x_scales[0].bitcast(I32)
 
-        for q in range(4):
-            nc.scalar.dma_start(out=x_sc[32 * q : 32 * q + 4, :].bitcast(I32), in_=s_view[4 * q : 4 * q + 4, :])
-        nc.sync.dma_start(out=w_raw[:], in_=w_view)
+        nc.sync.dma_start(out=w_raw[0][:], in_=w_view[:, :, 0:P])
         nc.sync.dma_start(out=x_codes[0][:].bitcast(I32), in_=x_view[:, 0:256])
+        for q in range(4):
+            nc.sync.dma_start(out=x_sc[32 * q : 32 * q + 4, :].bitcast(I32), in_=s_view[4 * q : 4 * q + 4, :])
         nc.sync.dma_start(offsets[:], slot)
         nc.sync.dma_start(out=win[0][:], in_=mem[0:P, :])
         nc.sync.dma_start(out=x_codes[1][:].bitcast(I32), in_=x_view[:, 256:512])
+        nc.sync.dma_start(out=w_raw[1][:], in_=w_view[:, :, P : 2 * P])
         nc.sync.dma_start(out=x_codes[2][:].bitcast(I32), in_=x_view[:, 512:1024])
         nc.sync.dma_start(out=win[1][:], in_=mem[P : 2 * P, :])
 
-        def product(b, c):
+        def product(b, c, y):
             lo, hi = chunks[c]
             acc = psum.tile([P, hi - lo], F32, name="acc%d_%d" % (b, c))
             nc.tensor.matmul_mx(out=acc[:], lhsT=w_codes[b][:].bitcast(FP8X4), lhsT_scale=w_sc[b][:],
                                 rhs=x_codes[c][:].bitcast(FP8X4), rhs_scale=x_sc[:, lo:hi], start=True, stop=True)
-            return acc
+            nc.scalar.activation(out=y, in_=acc[:], func=TANH)
 
-        for b in range(2):
-            nc.vector.tensor_copy(out=w_bf[b][:], in_=w_raw[:, :, b * P : (b + 1) * P].rearrange("p j w -> p w j"))
-        for b in range(2):
-            nc.vector.quantize_mx(out=w_codes[b][:].bitcast(FP8X4), scales=w_sc[b][:], in_=w_bf[b][:].rearrange("p w j -> p (w j)"))
+        nc.vector.tensor_copy(out=w_bf[0][:], in_=w_raw[0][:].rearrange("p j w -> p w j"))
+        nc.vector.quantize_mx(out=w_codes[0][:].bitcast(FP8X4), scales=w_sc[0][:], in_=w_bf[0][:].rearrange("p w j -> p (w j)"))
         y0 = [keep.tile([P, b - a], F32, name="y0_%d" % a) for a, b in chunks]
+        for c in range(2):
+            product(0, c, y0[c][:])
+        nc.vector.tensor_copy(win[0][:].indirect(offsets[:, 0:16]), y0[0][:])
+        nc.vector.tensor_copy(win[0][:].indirect(offsets[:, 16:32]), y0[1][:])
+        nc.scalar.copy(out=w_bf[1][:], in_=w_raw[1][:].rearrange("p j w -> p w j"))
+        nc.vector.quantize_mx(out=w_codes[1][:].bitcast(FP8X4), scales=w_sc[1][:], in_=w_bf[1][:].rearrange("p w j -> p (w j)"))
+        product(0, 2, y0[2][:])
+        nc.vector.tensor_copy(win[0][:].indirect(offsets[:, 32:64]), y0[2][:])
+        nc.sync.dma_start(out=out[0:P, :], in_=win[0][:])
         y1 = keep.tile([P, T], F32, name="y1")
         for c in range(3):
-            nc.scalar.activation(out=y0[c][:], in_=product(0, c)[:], func=TANH)
-        for c in range(3):
-            nc.scalar.activation(out=y1[:, chunks[c][0] : chunks[c][1]], in_=product(1, c)[:], func=TANH)
-        for c in range(3):
-            nc.vector.tensor_copy(win[0][:].indirect(offsets[:, chunks[c][0] // 16 : chunks[c][1] // 16]), y0[c][:])
-        nc.sync.dma_start(out=out[0:P, :], in_=win[0][:])
+            product(1, c, y1[:, chunks[c][0] : chunks[c][1]])
         nc.vector.tensor_copy(win[1][:].indirect(offsets[:]), y1[:])
         nc.sync.dma_start(out=out[P : 2 * P, :], in_=win[1][:])

@@ -11,9 +11,13 @@ U8 = mybir.dt.uint8
 FP8X4 = mybir.dt.float8_e4m3fn_x4
 TANH = mybir.ActivationFunctionType.Tanh
 
-K, T, N, U = 512, 1024, 256, 2048
+K, TOKENS, ROWS, SLOTS = 512, 1024, 256, 2048
+FLOPS = 2 * K * TOKENS * ROWS
+
 P = 128
-FLOPS = 2 * K * T * N
+PACK = 4
+GROUP = 16
+PIECES = ((0, 256), (256, 512), (512, 1024))
 
 
 def tile_picked_wkvput_tanh_l_kernel(tc, x_words, x_scales, mem, w1, slot, out):
@@ -22,51 +26,87 @@ def tile_picked_wkvput_tanh_l_kernel(tc, x_words, x_scales, mem, w1, slot, out):
         keep = ctx.enter_context(tc.tile_pool(name="keep", bufs=1))
         psum = ctx.enter_context(tc.psum_pool(name="psum", bufs=1))
 
-        chunks = [(0, 256), (256, 512), (512, 1024)]
-        offsets = keep.tile([P, T // 16], U16, name="offsets")
-        w_raw = [keep.tile([P, 4, P], F32, name="w_raw%d" % b) for b in range(2)]
-        w_bf = [keep.tile([P, P, 4], BF16, name="w_bf%d" % b, align_bytes=64) for b in range(2)]
+        offsets = keep.tile([P, TOKENS // GROUP], U16, name="offsets")
+        w_raw = [keep.tile([P, PACK, P], F32, name="w_raw%d" % b) for b in range(2)]
+        w_bf16 = [keep.tile([P, P, PACK], BF16, name="w_bf16_%d" % b, align_bytes=64) for b in range(2)]
         w_codes = [keep.tile([P, P], U32, name="w_codes%d" % b, align_bytes=64) for b in range(2)]
-        w_sc = [keep.tile([P, P], U8, name="w_sc%d" % b, align_bytes=64) for b in range(2)]
-        x_codes = [keep.tile([P, b - a], U32, name="x_codes%d" % a, align_bytes=64) for a, b in chunks]
-        x_sc = keep.tile([P, T], U8, name="x_sc", align_bytes=64)
-        win = [keep.tile([P, U], F32, name="win%d" % b) for b in range(2)]
-        w_view = w1.rearrange("(p j) n -> p j n", j=4)
-        x_view = x_words[0].rearrange("p n t -> p (n t)").bitcast(I32)
-        s_view = x_scales[0].bitcast(I32)
+        w_scale = [keep.tile([P, P], U8, name="w_scale%d" % b, align_bytes=64) for b in range(2)]
+        x_codes = [keep.tile([P, hi - lo], U32, name="x_codes%d" % lo, align_bytes=64) for lo, hi in PIECES]
+        x_scale = keep.tile([P, TOKENS], U8, name="x_scale", align_bytes=64)
+        window = [keep.tile([P, SLOTS], F32, name="window%d" % b) for b in range(2)]
+        y = [keep.tile([P, TOKENS], F32, name="y%d" % b) for b in range(2)]
 
-        nc.sync.dma_start(out=w_raw[0][:], in_=w_view[:, :, 0:P])
-        nc.sync.dma_start(out=x_codes[0][:].bitcast(I32), in_=x_view[:, 0:256])
-        for q in range(4):
-            nc.sync.dma_start(out=x_sc[32 * q : 32 * q + 4, :].bitcast(I32), in_=s_view[4 * q : 4 * q + 4, :])
+        w_rows = w1.rearrange("(p t) n -> p t n", t=PACK)
+        x_word_view = x_words[0].rearrange("p n t -> p (n t)").bitcast(I32)
+        x_scale_view = x_scales[0].bitcast(I32)
+
+        def load_weights(b):
+            nc.sync.dma_start(out=w_raw[b][:], in_=w_rows[:, :, b * P : (b + 1) * P])
+
+        def load_tokens(piece):
+            lo, hi = PIECES[piece]
+            nc.sync.dma_start(out=x_codes[piece][:].bitcast(I32), in_=x_word_view[:, lo:hi])
+
+        def load_window(b):
+            nc.sync.dma_start(out=window[b][:], in_=mem[b * P : (b + 1) * P, :])
+
+        def quantise_weights(b, copy):
+            copy(
+                out=w_bf16[b][:].rearrange("p (c i) t -> p c t i", i=PACK),
+                in_=w_raw[b][:].rearrange("p t (c i) -> p c t i", i=PACK),
+            )
+            nc.vector.quantize_mx(
+                out=w_codes[b][:].bitcast(FP8X4),
+                scales=w_scale[b][:],
+                in_=w_bf16[b][:].rearrange("p n t -> p (n t)"),
+            )
+
+        def project(b, piece):
+            lo, hi = PIECES[piece]
+            acc = psum.tile([P, hi - lo], F32, name="acc%d_%d" % (b, piece))
+            nc.tensor.matmul_mx(
+                out=acc[:],
+                lhsT=w_codes[b][:].bitcast(FP8X4),
+                lhsT_scale=w_scale[b][:],
+                rhs=x_codes[piece][:].bitcast(FP8X4),
+                rhs_scale=x_scale[:, lo:hi],
+                start=True,
+                stop=True,
+            )
+            nc.scalar.activation(out=y[b][:, lo:hi], in_=acc[:], func=TANH)
+
+        def scatter(b, lo, hi):
+            nc.vector.tensor_copy(window[b][:].indirect(offsets[:, lo // GROUP : hi // GROUP]), y[b][:, lo:hi])
+
+        def store_window(b):
+            nc.sync.dma_start(out=out[b * P : (b + 1) * P, :], in_=window[b][:])
+
+        load_weights(0)
+        load_tokens(0)
+        for quadrant in range(4):
+            nc.sync.dma_start(
+                out=x_scale[32 * quadrant : 32 * quadrant + 4, :].bitcast(I32),
+                in_=x_scale_view[4 * quadrant : 4 * quadrant + 4, :],
+            )
         nc.sync.dma_start(offsets[:], slot)
-        nc.sync.dma_start(out=win[0][:], in_=mem[0:P, :])
-        nc.sync.dma_start(out=x_codes[1][:].bitcast(I32), in_=x_view[:, 256:512])
-        nc.sync.dma_start(out=w_raw[1][:], in_=w_view[:, :, P : 2 * P])
-        nc.sync.dma_start(out=x_codes[2][:].bitcast(I32), in_=x_view[:, 512:1024])
-        nc.sync.dma_start(out=win[1][:], in_=mem[P : 2 * P, :])
+        load_window(0)
+        load_weights(1)
+        load_tokens(1)
+        load_window(1)
+        load_tokens(2)
 
-        def product(b, c, y):
-            lo, hi = chunks[c]
-            acc = psum.tile([P, hi - lo], F32, name="acc%d_%d" % (b, c))
-            nc.tensor.matmul_mx(out=acc[:], lhsT=w_codes[b][:].bitcast(FP8X4), lhsT_scale=w_sc[b][:],
-                                rhs=x_codes[c][:].bitcast(FP8X4), rhs_scale=x_sc[:, lo:hi], start=True, stop=True)
-            nc.scalar.activation(out=y, in_=acc[:], func=TANH)
-
-        nc.vector.tensor_copy(out=w_bf[0][:], in_=w_raw[0][:].rearrange("p j w -> p w j"))
-        nc.vector.quantize_mx(out=w_codes[0][:].bitcast(FP8X4), scales=w_sc[0][:], in_=w_bf[0][:].rearrange("p w j -> p (w j)"))
-        y0 = [keep.tile([P, b - a], F32, name="y0_%d" % a) for a, b in chunks]
-        for c in range(2):
-            product(0, c, y0[c][:])
-        nc.vector.tensor_copy(win[0][:].indirect(offsets[:, 0:16]), y0[0][:])
-        nc.vector.tensor_copy(win[0][:].indirect(offsets[:, 16:32]), y0[1][:])
-        nc.scalar.copy(out=w_bf[1][:], in_=w_raw[1][:].rearrange("p j w -> p w j"))
-        nc.vector.quantize_mx(out=w_codes[1][:].bitcast(FP8X4), scales=w_sc[1][:], in_=w_bf[1][:].rearrange("p w j -> p (w j)"))
-        product(0, 2, y0[2][:])
-        nc.vector.tensor_copy(win[0][:].indirect(offsets[:, 32:64]), y0[2][:])
-        nc.sync.dma_start(out=out[0:P, :], in_=win[0][:])
-        y1 = keep.tile([P, T], F32, name="y1")
-        for c in range(3):
-            product(1, c, y1[:, chunks[c][0] : chunks[c][1]])
-        nc.vector.tensor_copy(win[1][:].indirect(offsets[:]), y1[:])
-        nc.sync.dma_start(out=out[P : 2 * P, :], in_=win[1][:])
+        quantise_weights(0, nc.vector.tensor_copy)
+        project(0, 0)
+        scatter(0, *PIECES[0])
+        quantise_weights(1, nc.scalar.copy)
+        project(0, 1)
+        scatter(0, *PIECES[1])
+        project(1, 0)
+        project(1, 1)
+        scatter(1, PIECES[0][0], PIECES[1][1])
+        project(0, 2)
+        scatter(0, *PIECES[2])
+        store_window(0)
+        project(1, 2)
+        scatter(1, *PIECES[2])
+        store_window(1)

@@ -81,15 +81,17 @@ def tile_picked_wkvput_tanh_l_kernel(tc, x_words, x_scales, mem, w1, slot, out):
         def store_window(b):
             nc.sync.dma_start(out=out[b * P : (b + 1) * P, :], in_=window[b][:])
 
+        half = SLOTS // 4
         load_weights(0)
+        nc.scalar.dma_start(out=window[0][:, :half], in_=mem[:P, :half])
         load_tokens(0)
         for quadrant in range(4):
             nc.sync.dma_start(
                 out=x_scale[32 * quadrant : 32 * quadrant + 4, :].bitcast(I32),
                 in_=x_scale_view[4 * quadrant : 4 * quadrant + 4, :],
             )
+        nc.sync.dma_start(out=window[0][:, half:], in_=mem[:P, half:])
         nc.sync.dma_start(offsets[:], slot)
-        load_window(0)
         load_weights(1)
         load_tokens(1)
         load_window(1)

@@ -16,6 +16,7 @@ FLOPS = 2 * K * TOKENS * ROWS
 
 P = 128
 PACK = 4
+PLANE = 256
 GROUP = 16
 PIECES = ((0, 256), (256, 512), (512, 1024))
 
@@ -32,13 +33,13 @@ def tile_picked_wkvput_tanh_l_kernel(tc, x_words, x_scales, mem, w1, slot, out):
         w_codes = [keep.tile([P, P], U32, name="w_codes%d" % b, align_bytes=64) for b in range(2)]
         w_scale = [keep.tile([P, P], U8, name="w_scale%d" % b, align_bytes=64) for b in range(2)]
         x_codes = [keep.tile([P, hi - lo], U32, name="x_codes%d" % lo, align_bytes=64) for lo, hi in PIECES]
-        x_scale = keep.tile([P, TOKENS], U8, name="x_scale", align_bytes=64)
+        x_scale = keep.tile([P, PLANE], U8, name="x_scale", align_bytes=64)
         window = [keep.tile([P, SLOTS], F32, name="window%d" % b) for b in range(2)]
         y = [keep.tile([P, TOKENS], F32, name="y%d" % b) for b in range(2)]
 
         w_rows = w1.rearrange("(p t) n -> p t n", t=PACK)
         x_word_view = x_words[0].rearrange("p n t -> p (n t)").bitcast(I32)
-        x_scale_view = x_scales[0].bitcast(I32)
+        x_scale_view = x_scales[0].bitcast(I32).rearrange("r (a n) -> a r n", a=4)
 
         def load_weights(b):
             nc.sync.dma_start(out=w_raw[b][:], in_=w_rows[:, :, b * P : (b + 1) * P])
@@ -50,30 +51,34 @@ def tile_picked_wkvput_tanh_l_kernel(tc, x_words, x_scales, mem, w1, slot, out):
         def load_window(b):
             nc.sync.dma_start(out=window[b][:], in_=mem[b * P : (b + 1) * P, :])
 
-        def quantise_weights(b, copy):
+        def round_weights(b, copy, lo, hi):
             copy(
-                out=w_bf16[b][:].rearrange("p (c i) t -> p c t i", i=PACK),
-                in_=w_raw[b][:].rearrange("p t (c i) -> p c t i", i=PACK),
+                out=w_bf16[b][:, lo:hi, :].rearrange("p (c i) t -> p c t i", i=PACK),
+                in_=w_raw[b][:, :, lo:hi].rearrange("p t (c i) -> p c t i", i=PACK),
             )
+
+        def quantise_weights(b):
             nc.vector.quantize_mx(
                 out=w_codes[b][:].bitcast(FP8X4),
                 scales=w_scale[b][:],
                 in_=w_bf16[b][:].rearrange("p n t -> p (n t)"),
             )
 
-        def project(b, piece):
+        def project(b, piece, width):
             lo, hi = PIECES[piece]
-            acc = psum.tile([P, hi - lo], F32, name="acc%d_%d" % (b, piece))
-            nc.tensor.matmul_mx(
-                out=acc[:],
-                lhsT=w_codes[b][:].bitcast(FP8X4),
-                lhsT_scale=w_scale[b][:],
-                rhs=x_codes[piece][:].bitcast(FP8X4),
-                rhs_scale=x_scale[:, lo:hi],
-                start=True,
-                stop=True,
-            )
-            nc.scalar.activation(out=y[b][:, lo:hi], in_=acc[:], func=TANH)
+            for at in range(lo, hi, width):
+                plane, col = divmod(at, PLANE)
+                acc = psum.tile([P, width], F32, name="acc", bufs=8)
+                nc.tensor.matmul_mx(
+                    out=acc[:],
+                    lhsT=w_codes[b][:].bitcast(FP8X4),
+                    lhsT_scale=w_scale[b][:],
+                    rhs=x_codes[piece][:, at - lo : at - lo + width].bitcast(FP8X4),
+                    rhs_scale=x_scale[4 * plane :, col : col + width],
+                    start=True,
+                    stop=True,
+                )
+                nc.scalar.activation(out=y[b][:, at : at + width], in_=acc[:], func=TANH)
 
         def scatter(b, lo, hi):
             nc.vector.tensor_copy(window[b][:].indirect(offsets[:, lo // GROUP : hi // GROUP]), y[b][:, lo:hi])
@@ -87,8 +92,8 @@ def tile_picked_wkvput_tanh_l_kernel(tc, x_words, x_scales, mem, w1, slot, out):
         load_tokens(0)
         for quadrant in range(4):
             nc.sync.dma_start(
-                out=x_scale[32 * quadrant : 32 * quadrant + 4, :].bitcast(I32),
-                in_=x_scale_view[4 * quadrant : 4 * quadrant + 4, :],
+                out=x_scale[32 * quadrant : 32 * quadrant + 16, :].bitcast(I32),
+                in_=x_scale_view[:, 4 * quadrant : 4 * quadrant + 4, :],
             )
         nc.sync.dma_start(out=window[0][:, half:], in_=mem[:P, half:])
         nc.sync.dma_start(offsets[:], slot)
@@ -97,18 +102,21 @@ def tile_picked_wkvput_tanh_l_kernel(tc, x_words, x_scales, mem, w1, slot, out):
         load_window(1)
         load_tokens(2)
 
-        quantise_weights(0, nc.vector.tensor_copy)
-        project(0, 0)
+        round_weights(0, nc.vector.tensor_copy, 0, 96)
+        round_weights(0, nc.scalar.copy, 96, P)
+        quantise_weights(0)
+        project(0, 0, P)
         scatter(0, *PIECES[0])
-        quantise_weights(1, nc.scalar.copy)
-        project(0, 1)
+        round_weights(1, nc.scalar.copy, 0, P)
+        quantise_weights(1)
+        project(0, 1, PLANE)
         scatter(0, *PIECES[1])
-        project(1, 0)
-        project(1, 1)
+        project(1, 0, PLANE)
+        project(1, 1, PLANE)
         scatter(1, PIECES[0][0], PIECES[1][1])
-        project(0, 2)
+        project(0, 2, PLANE)
         scatter(0, *PIECES[2])
         store_window(0)
-        project(1, 2)
+        project(1, 2, PLANE)
         scatter(1, *PIECES[2])
         store_window(1)

@@ -28,13 +28,13 @@ def tile_picked_wkvput_tanh_l_kernel(tc, x_words, x_scales, mem, w1, slot, out):
         psum = ctx.enter_context(tc.psum_pool(name="psum", bufs=1))
 
         offsets = keep.tile([P, TOKENS // GROUP], U16, name="offsets")
-        w_raw = [keep.tile([P, PACK, P], F32, name="w_raw%d" % b) for b in range(2)]
+        w_raw = [keep.tile([P, PACK, P], F32, name="w_raw%d" % b, align_bytes=256) for b in range(2)]
         w_bf16 = [keep.tile([P, P, PACK], BF16, name="w_bf16_%d" % b, align_bytes=64) for b in range(2)]
         w_codes = [keep.tile([P, P], U32, name="w_codes%d" % b, align_bytes=64) for b in range(2)]
         w_scale = [keep.tile([P, P], U8, name="w_scale%d" % b, align_bytes=64) for b in range(2)]
-        x_codes = [keep.tile([P, hi - lo], U32, name="x_codes%d" % lo, align_bytes=64) for lo, hi in PIECES]
-        x_scale = keep.tile([P, PLANE], U8, name="x_scale", align_bytes=64)
-        window = [keep.tile([P, SLOTS], F32, name="window%d" % b) for b in range(2)]
+        x_codes = [keep.tile([P, hi - lo], U32, name="x_codes%d" % lo, align_bytes=256) for lo, hi in PIECES]
+        x_scale = keep.tile([P, PLANE], U8, name="x_scale", align_bytes=256)
+        window = [keep.tile([P, SLOTS], F32, name="window%d" % b, align_bytes=256) for b in range(2)]
         y = [keep.tile([P, TOKENS], F32, name="y%d" % b) for b in range(2)]
 
         w_rows = w1.rearrange("(p t) n -> p t n", t=PACK)

@@ -15,10 +15,19 @@ K, TOKENS, ROWS, SLOTS = 512, 1024, 256, 2048
 FLOPS = 2 * K * TOKENS * ROWS
 
 P = 128
+BLOCKS = ROWS // P
 PACK = 4
-PLANE = 256
 GROUP = 16
+QUADRANT = 32
+SCALE_ROWS = 4
+PLANE = 256
+SHORT_PASS = 128
+PSUM_BANKS = 8
+MX_ALIGN = 64
+DMA_ALIGN = 256
 PIECES = ((0, 256), (256, 512), (512, 1024))
+EARLY_COLUMNS = SLOTS // 4
+VECTOR_COLUMNS = 96
 
 
 def tile_picked_wkvput_tanh_l_kernel(tc, x_words, x_scales, mem, w1, slot, out):
@@ -27,19 +36,20 @@ def tile_picked_wkvput_tanh_l_kernel(tc, x_words, x_scales, mem, w1, slot, out):
         keep = ctx.enter_context(tc.tile_pool(name="keep", bufs=1))
         psum = ctx.enter_context(tc.psum_pool(name="psum", bufs=1))
 
-        offsets = keep.tile([P, TOKENS // GROUP], U16, name="offsets")
-        w_raw = [keep.tile([P, PACK, P], F32, name="w_raw%d" % b, align_bytes=256) for b in range(2)]
-        w_bf16 = [keep.tile([P, P, PACK], BF16, name="w_bf16_%d" % b, align_bytes=64) for b in range(2)]
-        w_codes = [keep.tile([P, P], U32, name="w_codes%d" % b, align_bytes=64) for b in range(2)]
-        w_scale = [keep.tile([P, P], U8, name="w_scale%d" % b, align_bytes=64) for b in range(2)]
-        x_codes = [keep.tile([P, hi - lo], U32, name="x_codes%d" % lo, align_bytes=256) for lo, hi in PIECES]
-        x_scale = keep.tile([P, PLANE], U8, name="x_scale", align_bytes=256)
-        window = [keep.tile([P, SLOTS], F32, name="window%d" % b, align_bytes=256) for b in range(2)]
-        y = [keep.tile([P, TOKENS], F32, name="y%d" % b) for b in range(2)]
+        blocks = range(BLOCKS)
+        offsets = keep.tile([P, TOKENS // GROUP], U16, name="offsets", align_bytes=DMA_ALIGN)
+        w_raw = [keep.tile([P, PACK, P], F32, name="w_raw%d" % b, align_bytes=DMA_ALIGN) for b in blocks]
+        w_bf16 = [keep.tile([P, P, PACK], BF16, name="w_bf16_%d" % b, align_bytes=MX_ALIGN) for b in blocks]
+        w_codes = [keep.tile([P, P], U32, name="w_codes%d" % b, align_bytes=MX_ALIGN) for b in blocks]
+        w_scale = [keep.tile([P, P], U8, name="w_scale%d" % b, align_bytes=MX_ALIGN) for b in blocks]
+        x_codes = [keep.tile([P, hi - lo], U32, name="x_codes%d" % lo, align_bytes=DMA_ALIGN) for lo, hi in PIECES]
+        x_scale = keep.tile([P, PLANE], U8, name="x_scale", align_bytes=DMA_ALIGN)
+        window = [keep.tile([P, SLOTS], F32, name="window%d" % b, align_bytes=DMA_ALIGN) for b in blocks]
+        y = [keep.tile([P, TOKENS], F32, name="y%d" % b) for b in blocks]
 
         w_rows = w1.rearrange("(p t) n -> p t n", t=PACK)
         x_word_view = x_words[0].rearrange("p n t -> p (n t)").bitcast(I32)
-        x_scale_view = x_scales[0].bitcast(I32).rearrange("r (a n) -> a r n", a=4)
+        x_scale_view = x_scales[0].bitcast(I32).rearrange("q (a n) -> a q n", a=TOKENS // PLANE)
 
         def load_weights(b):
             nc.sync.dma_start(out=w_raw[b][:], in_=w_rows[:, :, b * P : (b + 1) * P])
@@ -48,10 +58,17 @@ def tile_picked_wkvput_tanh_l_kernel(tc, x_words, x_scales, mem, w1, slot, out):
             lo, hi = PIECES[piece]
             nc.sync.dma_start(out=x_codes[piece][:].bitcast(I32), in_=x_word_view[:, lo:hi])
 
-        def load_window(b):
-            nc.sync.dma_start(out=window[b][:], in_=mem[b * P : (b + 1) * P, :])
+        def load_scales(quadrant):
+            first = QUADRANT * quadrant
+            nc.sync.dma_start(
+                out=x_scale[first : first + SCALE_ROWS * (TOKENS // PLANE), :].bitcast(I32),
+                in_=x_scale_view[:, SCALE_ROWS * quadrant : SCALE_ROWS * (quadrant + 1), :],
+            )
 
-        def round_weights(b, copy, lo, hi):
+        def load_window(queue, b, lo, hi):
+            queue.dma_start(out=window[b][:, lo:hi], in_=mem[b * P : (b + 1) * P, lo:hi])
+
+        def round_weights(copy, b, lo, hi):
             copy(
                 out=w_bf16[b][:, lo:hi, :].rearrange("p (c i) t -> p c t i", i=PACK),
                 in_=w_raw[b][:, :, lo:hi].rearrange("p t (c i) -> p c t i", i=PACK),
@@ -66,19 +83,19 @@ def tile_picked_wkvput_tanh_l_kernel(tc, x_words, x_scales, mem, w1, slot, out):
 
         def project(b, piece, width):
             lo, hi = PIECES[piece]
-            for at in range(lo, hi, width):
-                plane, col = divmod(at, PLANE)
-                acc = psum.tile([P, width], F32, name="acc", bufs=8)
+            for token in range(lo, hi, width):
+                plane, column = divmod(token, PLANE)
+                acc = psum.tile([P, width], F32, name="acc", bufs=PSUM_BANKS)
                 nc.tensor.matmul_mx(
                     out=acc[:],
                     lhsT=w_codes[b][:].bitcast(FP8X4),
                     lhsT_scale=w_scale[b][:],
-                    rhs=x_codes[piece][:, at - lo : at - lo + width].bitcast(FP8X4),
-                    rhs_scale=x_scale[4 * plane :, col : col + width],
+                    rhs=x_codes[piece][:, token - lo : token - lo + width].bitcast(FP8X4),
+                    rhs_scale=x_scale[SCALE_ROWS * plane :, column : column + width],
                     start=True,
                     stop=True,
                 )
-                nc.scalar.activation(out=y[b][:, at : at + width], in_=acc[:], func=TANH)
+                nc.scalar.activation(out=y[b][:, token : token + width], in_=acc[:], func=TANH)
 
         def scatter(b, lo, hi):
             nc.vector.tensor_copy(window[b][:].indirect(offsets[:, lo // GROUP : hi // GROUP]), y[b][:, lo:hi])
@@ -86,30 +103,26 @@ def tile_picked_wkvput_tanh_l_kernel(tc, x_words, x_scales, mem, w1, slot, out):
         def store_window(b):
             nc.sync.dma_start(out=out[b * P : (b + 1) * P, :], in_=window[b][:])
 
-        half = SLOTS // 4
         load_weights(0)
-        nc.scalar.dma_start(out=window[0][:, :half], in_=mem[:P, :half])
+        load_window(nc.scalar, 0, 0, EARLY_COLUMNS)
         load_tokens(0)
-        for quadrant in range(4):
-            nc.sync.dma_start(
-                out=x_scale[32 * quadrant : 32 * quadrant + 16, :].bitcast(I32),
-                in_=x_scale_view[:, 4 * quadrant : 4 * quadrant + 4, :],
-            )
-        nc.sync.dma_start(out=window[0][:, half:], in_=mem[:P, half:])
+        for quadrant in range(P // QUADRANT):
+            load_scales(quadrant)
+        load_window(nc.sync, 0, EARLY_COLUMNS, SLOTS)
         nc.sync.dma_start(offsets[:], slot)
         load_weights(1)
         load_tokens(1)
-        load_window(1)
+        load_window(nc.sync, 1, 0, SLOTS)
         load_tokens(2)
 
-        round_weights(0, nc.vector.tensor_copy, 0, 96)
-        round_weights(0, nc.scalar.copy, 96, P)
+        round_weights(nc.vector.tensor_copy, 0, 0, VECTOR_COLUMNS)
+        round_weights(nc.scalar.copy, 0, VECTOR_COLUMNS, P)
         quantise_weights(0)
-        project(0, 0, P)
+        project(0, 0, SHORT_PASS)
         scatter(0, *PIECES[0])
-        round_weights(1, nc.scalar.copy, 0, P)
+        round_weights(nc.scalar.copy, 1, 0, P)
         quantise_weights(1)
-        project(0, 1, PLANE)
+        project(0, 1, SHORT_PASS)
         scatter(0, *PIECES[1])
         project(1, 0, PLANE)
         project(1, 1, PLANE)

@@ -20,12 +20,14 @@ PACK = 4
 GROUP = 16
 QUADRANT = 32
 SCALE_ROWS = 4
-PLANE = 256
+STORE_PARTS = 4
+HALF = TOKENS // 2
+LONG_PASS = 256
 SHORT_PASS = 128
 PSUM_BANKS = 8
 MX_ALIGN = 64
 DMA_ALIGN = 256
-PIECES = ((0, 256), (256, 512), (512, 1024))
+PIECES = ((0, 256), (256, 512), (512, 768), (768, 1024))
 EARLY_COLUMNS = SLOTS // 4
 VECTOR_COLUMNS = 96
 
@@ -43,13 +45,13 @@ def tile_picked_wkvput_tanh_l_kernel(tc, x_words, x_scales, mem, w1, slot, out):
         w_codes = [keep.tile([P, P], U32, name="w_codes%d" % b, align_bytes=MX_ALIGN) for b in blocks]
         w_scale = [keep.tile([P, P], U8, name="w_scale%d" % b, align_bytes=MX_ALIGN) for b in blocks]
         x_codes = [keep.tile([P, hi - lo], U32, name="x_codes%d" % lo, align_bytes=DMA_ALIGN) for lo, hi in PIECES]
-        x_scale = keep.tile([P, PLANE], U8, name="x_scale", align_bytes=DMA_ALIGN)
+        x_scale = [keep.tile([P, HALF], U8, name="x_scale%d" % h, align_bytes=DMA_ALIGN) for h in range(2)]
         window = [keep.tile([P, SLOTS], F32, name="window%d" % b, align_bytes=DMA_ALIGN) for b in blocks]
         y = [keep.tile([P, TOKENS], F32, name="y%d" % b) for b in blocks]
 
         w_rows = w1.rearrange("(p t) n -> p t n", t=PACK)
         x_word_view = x_words[0].rearrange("p n t -> p (n t)").bitcast(I32)
-        x_scale_view = x_scales[0].bitcast(I32).rearrange("q (a n) -> a q n", a=TOKENS // PLANE)
+        x_scale_view = x_scales[0].bitcast(I32).rearrange("q (h n) -> h q n", h=2)
 
         def load_weights(b):
             nc.sync.dma_start(out=w_raw[b][:], in_=w_rows[:, :, b * P : (b + 1) * P])
@@ -58,12 +60,13 @@ def tile_picked_wkvput_tanh_l_kernel(tc, x_words, x_scales, mem, w1, slot, out):
             lo, hi = PIECES[piece]
             nc.sync.dma_start(out=x_codes[piece][:].bitcast(I32), in_=x_word_view[:, lo:hi])
 
-        def load_scales(quadrant):
-            first = QUADRANT * quadrant
-            nc.sync.dma_start(
-                out=x_scale[first : first + SCALE_ROWS * (TOKENS // PLANE), :].bitcast(I32),
-                in_=x_scale_view[:, SCALE_ROWS * quadrant : SCALE_ROWS * (quadrant + 1), :],
-            )
+        def load_scales(half):
+            for quadrant in range(P // QUADRANT):
+                first = QUADRANT * quadrant
+                nc.sync.dma_start(
+                    out=x_scale[half][first : first + SCALE_ROWS, :].bitcast(I32),
+                    in_=x_scale_view[half, SCALE_ROWS * quadrant : SCALE_ROWS * (quadrant + 1), :],
+                )
 
         def load_window(queue, b, lo, hi):
             queue.dma_start(out=window[b][:, lo:hi], in_=mem[b * P : (b + 1) * P, lo:hi])
@@ -84,14 +87,14 @@ def tile_picked_wkvput_tanh_l_kernel(tc, x_words, x_scales, mem, w1, slot, out):
         def project(b, piece, width):
             lo, hi = PIECES[piece]
             for token in range(lo, hi, width):
-                plane, column = divmod(token, PLANE)
+                half, column = divmod(token, HALF)
                 acc = psum.tile([P, width], F32, name="acc", bufs=PSUM_BANKS)
                 nc.tensor.matmul_mx(
                     out=acc[:],
                     lhsT=w_codes[b][:].bitcast(FP8X4),
                     lhsT_scale=w_scale[b][:],
                     rhs=x_codes[piece][:, token - lo : token - lo + width].bitcast(FP8X4),
-                    rhs_scale=x_scale[SCALE_ROWS * plane :, column : column + width],
+                    rhs_scale=x_scale[half][:, column : column + width],
                     start=True,
                     stop=True,
                 )
@@ -100,20 +103,23 @@ def tile_picked_wkvput_tanh_l_kernel(tc, x_words, x_scales, mem, w1, slot, out):
         def scatter(b, lo, hi):
             nc.vector.tensor_copy(window[b][:].indirect(offsets[:, lo // GROUP : hi // GROUP]), y[b][:, lo:hi])
 
-        def store_window(b):
-            nc.sync.dma_start(out=out[b * P : (b + 1) * P, :], in_=window[b][:])
+        def store_window(b, parts):
+            for lo in range(0, SLOTS, SLOTS // parts):
+                columns = slice(lo, lo + SLOTS // parts)
+                nc.sync.dma_start(out=out[b * P : (b + 1) * P, columns], in_=window[b][:, columns])
 
         load_weights(0)
         load_window(nc.scalar, 0, 0, EARLY_COLUMNS)
         load_tokens(0)
-        for quadrant in range(P // QUADRANT):
-            load_scales(quadrant)
+        load_scales(0)
         load_window(nc.sync, 0, EARLY_COLUMNS, SLOTS)
         nc.sync.dma_start(offsets[:], slot)
         load_weights(1)
         load_tokens(1)
         load_window(nc.sync, 1, 0, SLOTS)
+        load_scales(1)
         load_tokens(2)
+        load_tokens(3)
 
         round_weights(nc.vector.tensor_copy, 0, 0, VECTOR_COLUMNS)
         round_weights(nc.scalar.copy, 0, VECTOR_COLUMNS, P)
@@ -124,12 +130,14 @@ def tile_picked_wkvput_tanh_l_kernel(tc, x_words, x_scales, mem, w1, slot, out):
         quantise_weights(1)
         project(0, 1, SHORT_PASS)
         scatter(0, *PIECES[1])
-        project(1, 0, PLANE)
-        project(1, 1, PLANE)
-        scatter(1, PIECES[0][0], PIECES[1][1])
-        project(0, 2, PLANE)
-        scatter(0, *PIECES[2])
-        store_window(0)
-        project(1, 2, PLANE)
-        scatter(1, *PIECES[2])
-        store_window(1)
+        project(1, 0, LONG_PASS)
+        project(1, 1, LONG_PASS)
+        scatter(1, 0, HALF)
+        project(0, 2, LONG_PASS)
+        project(0, 3, LONG_PASS)
+        scatter(0, HALF, TOKENS)
+        store_window(0, STORE_PARTS)
+        project(1, 2, LONG_PASS)
+        project(1, 3, LONG_PASS)
+        scatter(1, HALF, TOKENS)
+        store_window(1, 1)

@@ -19,6 +19,8 @@ BLOCKS = ROWS // P
 PACK = 4
 GROUP = 16
 QUADRANT = 32
+QUADRANTS = P // QUADRANT
+AHEAD = 1
 SCALE_ROWS = 4
 STORE_PARTS = 4
 HALF = TOKENS // 2
@@ -60,8 +62,8 @@ def tile_picked_wkvput_tanh_l_kernel(tc, x_words, x_scales, mem, w1, slot, out):
             lo, hi = PIECES[piece]
             nc.sync.dma_start(out=x_codes[piece][:].bitcast(I32), in_=x_word_view[:, lo:hi])
 
-        def load_scales(half):
-            for quadrant in range(P // QUADRANT):
+        def load_scales(half, quadrants):
+            for quadrant in quadrants:
                 first = QUADRANT * quadrant
                 nc.sync.dma_start(
                     out=x_scale[half][first : first + SCALE_ROWS, :].bitcast(I32),
@@ -111,13 +113,14 @@ def tile_picked_wkvput_tanh_l_kernel(tc, x_words, x_scales, mem, w1, slot, out):
         load_weights(0)
         load_window(nc.scalar, 0, 0, EARLY_COLUMNS)
         load_tokens(0)
-        load_scales(0)
+        load_scales(0, range(QUADRANTS))
         load_window(nc.sync, 0, EARLY_COLUMNS, SLOTS)
         nc.sync.dma_start(offsets[:], slot)
+        load_scales(1, range(AHEAD))
         load_weights(1)
         load_tokens(1)
         load_window(nc.sync, 1, 0, SLOTS)
-        load_scales(1)
+        load_scales(1, range(AHEAD, QUADRANTS))
         load_tokens(2)
         load_tokens(3)
 

@@ -10,6 +10,7 @@ U16 = mybir.dt.uint16
 U8 = mybir.dt.uint8
 FP8X4 = mybir.dt.float8_e4m3fn_x4
 TANH = mybir.ActivationFunctionType.Tanh
+COPY = mybir.ActivationFunctionType.Copy
 
 K, TOKENS, ROWS, SLOTS = 512, 1024, 256, 2048
 FLOPS = 2 * K * TOKENS * ROWS
@@ -20,18 +21,15 @@ PACK = 4
 GROUP = 16
 QUADRANT = 32
 QUADRANTS = P // QUADRANT
-AHEAD = 1
 SCALE_ROWS = 4
-STORE_PARTS = 4
 HALF = TOKENS // 2
-LONG_PASS = 256
-SHORT_PASS = 128
+PASS = 256
 PSUM_BANKS = 8
 MX_ALIGN = 64
 DMA_ALIGN = 256
-PIECES = ((0, 256), (256, 512), (512, 768), (768, 1024))
-EARLY_COLUMNS = SLOTS // 4
 VECTOR_COLUMNS = 96
+VECTOR_ENTRIES = 448
+SCALAR_CUT = 704
 
 
 def tile_picked_wkvput_tanh_l_kernel(tc, x_words, x_scales, mem, w1, slot, out):
@@ -41,42 +39,39 @@ def tile_picked_wkvput_tanh_l_kernel(tc, x_words, x_scales, mem, w1, slot, out):
         psum = ctx.enter_context(tc.psum_pool(name="psum", bufs=1))
 
         blocks = range(BLOCKS)
+        halves = range(2)
         offsets = keep.tile([P, TOKENS // GROUP], U16, name="offsets", align_bytes=DMA_ALIGN)
-        w_raw = [keep.tile([P, PACK, P], F32, name="w_raw%d" % b, align_bytes=DMA_ALIGN) for b in blocks]
+        w_raw = keep.tile([P, PACK, ROWS], F32, name="w_raw", align_bytes=DMA_ALIGN)
         w_bf16 = [keep.tile([P, P, PACK], BF16, name="w_bf16_%d" % b, align_bytes=MX_ALIGN) for b in blocks]
         w_codes = [keep.tile([P, P], U32, name="w_codes%d" % b, align_bytes=MX_ALIGN) for b in blocks]
         w_scale = [keep.tile([P, P], U8, name="w_scale%d" % b, align_bytes=MX_ALIGN) for b in blocks]
-        x_codes = [keep.tile([P, hi - lo], U32, name="x_codes%d" % lo, align_bytes=DMA_ALIGN) for lo, hi in PIECES]
-        x_scale = [keep.tile([P, HALF], U8, name="x_scale%d" % h, align_bytes=DMA_ALIGN) for h in range(2)]
+        x_codes = [keep.tile([P, HALF], U32, name="x_codes%d" % h, align_bytes=DMA_ALIGN) for h in halves]
+        x_scale = keep.tile([P, TOKENS], U8, name="x_scale", align_bytes=DMA_ALIGN)
         window = [keep.tile([P, SLOTS], F32, name="window%d" % b, align_bytes=DMA_ALIGN) for b in blocks]
         y = [keep.tile([P, TOKENS], F32, name="y%d" % b) for b in blocks]
 
         w_rows = w1.rearrange("(p t) n -> p t n", t=PACK)
         x_word_view = x_words[0].rearrange("p n t -> p (n t)").bitcast(I32)
-        x_scale_view = x_scales[0].bitcast(I32).rearrange("q (h n) -> h q n", h=2)
+        x_scale_view = x_scales[0].bitcast(I32)
 
-        def load_weights(b):
-            nc.sync.dma_start(out=w_raw[b][:], in_=w_rows[:, :, b * P : (b + 1) * P])
+        def load_tokens(half):
+            nc.sync.dma_start(out=x_codes[half][:].bitcast(I32), in_=x_word_view[:, half * HALF : (half + 1) * HALF])
 
-        def load_tokens(piece):
-            lo, hi = PIECES[piece]
-            nc.sync.dma_start(out=x_codes[piece][:].bitcast(I32), in_=x_word_view[:, lo:hi])
-
-        def load_scales(half, quadrants):
-            for quadrant in quadrants:
+        def load_scales():
+            for quadrant in range(QUADRANTS):
                 first = QUADRANT * quadrant
                 nc.sync.dma_start(
-                    out=x_scale[half][first : first + SCALE_ROWS, :].bitcast(I32),
-                    in_=x_scale_view[half, SCALE_ROWS * quadrant : SCALE_ROWS * (quadrant + 1), :],
+                    out=x_scale[first : first + SCALE_ROWS, :].bitcast(I32),
+                    in_=x_scale_view[SCALE_ROWS * quadrant : SCALE_ROWS * (quadrant + 1), :],
                 )
 
-        def load_window(queue, b, lo, hi):
-            queue.dma_start(out=window[b][:, lo:hi], in_=mem[b * P : (b + 1) * P, lo:hi])
+        def load_window(b):
+            nc.sync.dma_start(out=window[b][:], in_=mem[b * P : (b + 1) * P, :])
 
         def round_weights(copy, b, lo, hi):
             copy(
                 out=w_bf16[b][:, lo:hi, :].rearrange("p (c i) t -> p c t i", i=PACK),
-                in_=w_raw[b][:, :, lo:hi].rearrange("p t (c i) -> p c t i", i=PACK),
+                in_=w_raw[:, :, b * P + lo : b * P + hi].rearrange("p t (c i) -> p c t i", i=PACK),
             )
 
         def quantise_weights(b):
@@ -86,61 +81,53 @@ def tile_picked_wkvput_tanh_l_kernel(tc, x_words, x_scales, mem, w1, slot, out):
                 in_=w_bf16[b][:].rearrange("p n t -> p (n t)"),
             )
 
-        def project(b, piece, width):
-            lo, hi = PIECES[piece]
-            for token in range(lo, hi, width):
-                half, column = divmod(token, HALF)
-                acc = psum.tile([P, width], F32, name="acc", bufs=PSUM_BANKS)
+        def project(b, half):
+            for column in range(0, HALF, PASS):
+                token = half * HALF + column
+                acc = psum.tile([P, PASS], F32, name="acc", bufs=PSUM_BANKS)
                 nc.tensor.matmul_mx(
                     out=acc[:],
                     lhsT=w_codes[b][:].bitcast(FP8X4),
                     lhsT_scale=w_scale[b][:],
-                    rhs=x_codes[piece][:, token - lo : token - lo + width].bitcast(FP8X4),
-                    rhs_scale=x_scale[half][:, column : column + width],
+                    rhs=x_codes[half][:, column : column + PASS].bitcast(FP8X4),
+                    rhs_scale=x_scale[:, token : token + PASS],
                     start=True,
                     stop=True,
                 )
-                nc.scalar.activation(out=y[b][:, token : token + width], in_=acc[:], func=TANH)
+                nc.scalar.activation(out=y[b][:, token : token + PASS], in_=acc[:], func=TANH)
 
-        def scatter(b, lo, hi):
-            nc.vector.tensor_copy(window[b][:].indirect(offsets[:, lo // GROUP : hi // GROUP]), y[b][:, lo:hi])
+        def target(b, lo, hi):
+            return window[b][:].indirect(offsets[:, lo // GROUP : hi // GROUP])
 
-        def store_window(b, parts):
-            for lo in range(0, SLOTS, SLOTS // parts):
-                columns = slice(lo, lo + SLOTS // parts)
-                nc.sync.dma_start(out=out[b * P : (b + 1) * P, columns], in_=window[b][:, columns])
+        def vector_scatter(b, lo, hi):
+            nc.vector.tensor_copy(target(b, lo, hi), y[b][:, lo:hi])
 
-        load_weights(0)
-        load_window(nc.scalar, 0, 0, EARLY_COLUMNS)
+        def scalar_scatter(b, lo, hi):
+            nc.scalar.activation(out=target(b, lo, hi), in_=y[b][:, lo:hi], func=COPY)
+
+        def store_window(b):
+            nc.sync.dma_start(out=out[b * P : (b + 1) * P, :], in_=window[b][:])
+
+        nc.sync.dma_start(out=w_raw[:], in_=w_rows)
         load_tokens(0)
-        load_scales(0, range(QUADRANTS))
-        load_window(nc.sync, 0, EARLY_COLUMNS, SLOTS)
+        load_scales()
         nc.sync.dma_start(offsets[:], slot)
-        load_scales(1, range(AHEAD))
-        load_weights(1)
+        load_window(0)
         load_tokens(1)
-        load_window(nc.sync, 1, 0, SLOTS)
-        load_scales(1, range(AHEAD, QUADRANTS))
-        load_tokens(2)
-        load_tokens(3)
+        load_window(1)
 
         round_weights(nc.vector.tensor_copy, 0, 0, VECTOR_COLUMNS)
         round_weights(nc.scalar.copy, 0, VECTOR_COLUMNS, P)
+        round_weights(nc.vector.tensor_copy, 1, 0, P)
         quantise_weights(0)
-        project(0, 0, SHORT_PASS)
-        scatter(0, *PIECES[0])
-        round_weights(nc.scalar.copy, 1, 0, P)
         quantise_weights(1)
-        project(0, 1, SHORT_PASS)
-        scatter(0, *PIECES[1])
-        project(1, 0, LONG_PASS)
-        project(1, 1, LONG_PASS)
-        scatter(1, 0, HALF)
-        project(0, 2, LONG_PASS)
-        project(0, 3, LONG_PASS)
-        scatter(0, HALF, TOKENS)
-        store_window(0, STORE_PARTS)
-        project(1, 2, LONG_PASS)
-        project(1, 3, LONG_PASS)
-        scatter(1, HALF, TOKENS)
-        store_window(1, 1)
+        project(0, 0)
+        vector_scatter(0, 0, VECTOR_ENTRIES)
+        project(1, 0)
+        project(1, 1)
+        project(0, 1)
+        vector_scatter(1, 0, TOKENS)
+        scalar_scatter(0, VECTOR_ENTRIES, SCALAR_CUT)
+        scalar_scatter(0, SCALAR_CUT, TOKENS)
+        store_window(0)
+        store_window(1)

@@ -22,14 +22,15 @@ GROUP = 16
 QUADRANT = 32
 QUADRANTS = P // QUADRANT
 SCALE_ROWS = 4
-HALF = TOKENS // 2
 PASS = 256
+EARLY = 384
+PIECES = ((0, EARLY), (EARLY, TOKENS))
+PLANES = TOKENS // PASS
 PSUM_BANKS = 8
 MX_ALIGN = 64
 DMA_ALIGN = 256
 VECTOR_COLUMNS = 96
-VECTOR_ENTRIES = 448
-SCALAR_CUT = 704
+SCALAR_CUT = 768
 
 
 def tile_picked_wkvput_tanh_l_kernel(tc, x_words, x_scales, mem, w1, slot, out):
@@ -39,30 +40,30 @@ def tile_picked_wkvput_tanh_l_kernel(tc, x_words, x_scales, mem, w1, slot, out):
         psum = ctx.enter_context(tc.psum_pool(name="psum", bufs=1))
 
         blocks = range(BLOCKS)
-        halves = range(2)
         offsets = keep.tile([P, TOKENS // GROUP], U16, name="offsets", align_bytes=DMA_ALIGN)
         w_raw = keep.tile([P, PACK, ROWS], F32, name="w_raw", align_bytes=DMA_ALIGN)
         w_bf16 = [keep.tile([P, P, PACK], BF16, name="w_bf16_%d" % b, align_bytes=MX_ALIGN) for b in blocks]
         w_codes = [keep.tile([P, P], U32, name="w_codes%d" % b, align_bytes=MX_ALIGN) for b in blocks]
         w_scale = [keep.tile([P, P], U8, name="w_scale%d" % b, align_bytes=MX_ALIGN) for b in blocks]
-        x_codes = [keep.tile([P, HALF], U32, name="x_codes%d" % h, align_bytes=DMA_ALIGN) for h in halves]
-        x_scale = keep.tile([P, TOKENS], U8, name="x_scale", align_bytes=DMA_ALIGN)
+        x_codes = [keep.tile([P, hi - lo], U32, name="x_codes%d" % lo, align_bytes=DMA_ALIGN) for lo, hi in PIECES]
+        x_scale = keep.tile([P, PASS], U8, name="x_scale", align_bytes=DMA_ALIGN)
         window = [keep.tile([P, SLOTS], F32, name="window%d" % b, align_bytes=DMA_ALIGN) for b in blocks]
         y = [keep.tile([P, TOKENS], F32, name="y%d" % b) for b in blocks]
 
         w_rows = w1.rearrange("(p t) n -> p t n", t=PACK)
         x_word_view = x_words[0].rearrange("p n t -> p (n t)").bitcast(I32)
-        x_scale_view = x_scales[0].bitcast(I32)
+        x_scale_view = x_scales[0].bitcast(I32).rearrange("q (a n) -> a q n", a=PLANES)
 
-        def load_tokens(half):
-            nc.sync.dma_start(out=x_codes[half][:].bitcast(I32), in_=x_word_view[:, half * HALF : (half + 1) * HALF])
+        def load_tokens(piece):
+            lo, hi = PIECES[piece]
+            nc.sync.dma_start(out=x_codes[piece][:].bitcast(I32), in_=x_word_view[:, lo:hi])
 
         def load_scales():
             for quadrant in range(QUADRANTS):
                 first = QUADRANT * quadrant
                 nc.sync.dma_start(
-                    out=x_scale[first : first + SCALE_ROWS, :].bitcast(I32),
-                    in_=x_scale_view[SCALE_ROWS * quadrant : SCALE_ROWS * (quadrant + 1), :],
+                    out=x_scale[first : first + PLANES * SCALE_ROWS, :].bitcast(I32),
+                    in_=x_scale_view[:, SCALE_ROWS * quadrant : SCALE_ROWS * (quadrant + 1), :],
                 )
 
         def load_window(b):
@@ -81,20 +82,25 @@ def tile_picked_wkvput_tanh_l_kernel(tc, x_words, x_scales, mem, w1, slot, out):
                 in_=w_bf16[b][:].rearrange("p n t -> p (n t)"),
             )
 
-        def project(b, half):
-            for column in range(0, HALF, PASS):
-                token = half * HALF + column
-                acc = psum.tile([P, PASS], F32, name="acc", bufs=PSUM_BANKS)
+        def project(b, lo, hi):
+            piece = 0 if lo < EARLY else 1
+            first = PIECES[piece][0]
+            token = lo
+            while token < hi:
+                plane, column = divmod(token, PASS)
+                width = min(PASS - column, hi - token)
+                acc = psum.tile([P, width], F32, name="acc", bufs=PSUM_BANKS)
                 nc.tensor.matmul_mx(
                     out=acc[:],
                     lhsT=w_codes[b][:].bitcast(FP8X4),
                     lhsT_scale=w_scale[b][:],
-                    rhs=x_codes[half][:, column : column + PASS].bitcast(FP8X4),
-                    rhs_scale=x_scale[:, token : token + PASS],
+                    rhs=x_codes[piece][:, token - first : token - first + width].bitcast(FP8X4),
+                    rhs_scale=x_scale[SCALE_ROWS * plane :, column : column + width],
                     start=True,
                     stop=True,
                 )
-                nc.scalar.activation(out=y[b][:, token : token + PASS], in_=acc[:], func=TANH)
+                nc.scalar.activation(out=y[b][:, token : token + width], in_=acc[:], func=TANH)
+                token = token + width
 
         def target(b, lo, hi):
             return window[b][:].indirect(offsets[:, lo // GROUP : hi // GROUP])
@@ -118,16 +124,16 @@ def tile_picked_wkvput_tanh_l_kernel(tc, x_words, x_scales, mem, w1, slot, out):
 
         round_weights(nc.vector.tensor_copy, 0, 0, VECTOR_COLUMNS)
         round_weights(nc.scalar.copy, 0, VECTOR_COLUMNS, P)
-        round_weights(nc.vector.tensor_copy, 1, 0, P)
         quantise_weights(0)
+        project(0, 0, EARLY)
+        round_weights(nc.vector.tensor_copy, 1, 0, P)
         quantise_weights(1)
-        project(0, 0)
-        vector_scatter(0, 0, VECTOR_ENTRIES)
-        project(1, 0)
-        project(1, 1)
-        project(0, 1)
+        vector_scatter(0, 0, EARLY)
+        project(1, 0, EARLY)
+        project(1, EARLY, TOKENS)
+        project(0, EARLY, TOKENS)
         vector_scatter(1, 0, TOKENS)
-        scalar_scatter(0, VECTOR_ENTRIES, SCALAR_CUT)
+        scalar_scatter(0, EARLY, SCALAR_CUT)
         scalar_scatter(0, SCALAR_CUT, TOKENS)
         store_window(0)
         store_window(1)

@@ -58,10 +58,10 @@ def tile_picked_wkvput_tanh_l_kernel(tc, x_words, x_scales, mem, w1, slot, out):
             lo, hi = PIECES[piece]
             nc.sync.dma_start(out=x_codes[piece][:].bitcast(I32), in_=x_word_view[:, lo:hi])
 
-        def load_scales():
-            for quadrant in range(QUADRANTS):
+        def load_scales(queue, quadrants):
+            for quadrant in quadrants:
                 first = QUADRANT * quadrant
-                nc.sync.dma_start(
+                queue.dma_start(
                     out=x_scale[first : first + PLANES * SCALE_ROWS, :].bitcast(I32),
                     in_=x_scale_view[:, SCALE_ROWS * quadrant : SCALE_ROWS * (quadrant + 1), :],
                 )
@@ -115,9 +115,10 @@ def tile_picked_wkvput_tanh_l_kernel(tc, x_words, x_scales, mem, w1, slot, out):
             nc.sync.dma_start(out=out[b * P : (b + 1) * P, :], in_=window[b][:])
 
         nc.sync.dma_start(out=w_raw[:], in_=w_rows)
-        load_tokens(0)
-        load_scales()
+        load_scales(nc.sync, range(1))
+        load_scales(nc.scalar, range(1, QUADRANTS))
         nc.sync.dma_start(offsets[:], slot)
+        load_tokens(0)
         load_window(0)
         load_tokens(1)
         load_window(1)

@@ -29,7 +29,8 @@ PLANES = TOKENS // PASS
 PSUM_BANKS = 8
 MX_ALIGN = 64
 DMA_ALIGN = 256
-VECTOR_COLUMNS = 96
+VECTOR_COLUMNS = 64
+SHORT_PASS = 128
 SCALAR_CUT = 768
 
 
@@ -82,13 +83,13 @@ def tile_picked_wkvput_tanh_l_kernel(tc, x_words, x_scales, mem, w1, slot, out):
                 in_=w_bf16[b][:].rearrange("p n t -> p (n t)"),
             )
 
-        def project(b, lo, hi):
+        def project(b, lo, hi, widest):
             piece = 0 if lo < EARLY else 1
             first = PIECES[piece][0]
             token = lo
             while token < hi:
                 plane, column = divmod(token, PASS)
-                width = min(PASS - column, hi - token)
+                width = min(widest, PASS - column, hi - token)
                 acc = psum.tile([P, width], F32, name="acc", bufs=PSUM_BANKS)
                 nc.tensor.matmul_mx(
                     out=acc[:],
@@ -126,13 +127,13 @@ def tile_picked_wkvput_tanh_l_kernel(tc, x_words, x_scales, mem, w1, slot, out):
         round_weights(nc.vector.tensor_copy, 0, 0, VECTOR_COLUMNS)
         round_weights(nc.scalar.copy, 0, VECTOR_COLUMNS, P)
         quantise_weights(0)
-        project(0, 0, EARLY)
-        round_weights(nc.vector.tensor_copy, 1, 0, P)
+        round_weights(nc.scalar.copy, 1, 0, P)
+        project(0, 0, EARLY, SHORT_PASS)
         quantise_weights(1)
         vector_scatter(0, 0, EARLY)
-        project(1, 0, EARLY)
-        project(1, EARLY, TOKENS)
-        project(0, EARLY, TOKENS)
+        project(1, 0, EARLY, PASS)
+        project(1, EARLY, TOKENS, PASS)
+        project(0, EARLY, TOKENS, PASS)
         vector_scatter(1, 0, TOKENS)
         scalar_scatter(0, EARLY, SCALAR_CUT)
         scalar_scatter(0, SCALAR_CUT, TOKENS)

@@ -25,7 +25,7 @@ SCALE_ROWS = 4
 PASS = 256
 EARLY = 384
 PIECES = ((0, EARLY), (EARLY, TOKENS))
-PLANES = TOKENS // PASS
+PLANES = 2
 PSUM_BANKS = 8
 MX_ALIGN = 64
 DMA_ALIGN = 256
@@ -47,24 +47,24 @@ def tile_picked_wkvput_tanh_l_kernel(tc, x_words, x_scales, mem, w1, slot, out):
         w_codes = [keep.tile([P, P], U32, name="w_codes%d" % b, align_bytes=MX_ALIGN) for b in blocks]
         w_scale = [keep.tile([P, P], U8, name="w_scale%d" % b, align_bytes=MX_ALIGN) for b in blocks]
         x_codes = [keep.tile([P, hi - lo], U32, name="x_codes%d" % lo, align_bytes=DMA_ALIGN) for lo, hi in PIECES]
-        x_scale = keep.tile([P, PASS], U8, name="x_scale", align_bytes=DMA_ALIGN)
+        x_scale = [keep.tile([P, PASS], U8, name="x_scale%d" % h, align_bytes=DMA_ALIGN) for h in range(2)]
         window = [keep.tile([P, SLOTS], F32, name="window%d" % b, align_bytes=DMA_ALIGN) for b in blocks]
         y = [keep.tile([P, TOKENS], F32, name="y%d" % b) for b in blocks]
 
         w_rows = w1.rearrange("(p t) n -> p t n", t=PACK)
         x_word_view = x_words[0].rearrange("p n t -> p (n t)").bitcast(I32)
-        x_scale_view = x_scales[0].bitcast(I32).rearrange("q (a n) -> a q n", a=PLANES)
+        x_scale_view = x_scales[0].bitcast(I32).rearrange("q (h a n) -> h a q n", h=2, a=PLANES)
 
         def load_tokens(piece):
             lo, hi = PIECES[piece]
             nc.sync.dma_start(out=x_codes[piece][:].bitcast(I32), in_=x_word_view[:, lo:hi])
 
-        def load_scales(queue, quadrants):
+        def load_scales(queue, half, quadrants):
             for quadrant in quadrants:
                 first = QUADRANT * quadrant
                 queue.dma_start(
-                    out=x_scale[first : first + PLANES * SCALE_ROWS, :].bitcast(I32),
-                    in_=x_scale_view[:, SCALE_ROWS * quadrant : SCALE_ROWS * (quadrant + 1), :],
+                    out=x_scale[half][first : first + PLANES * SCALE_ROWS, :].bitcast(I32),
+                    in_=x_scale_view[half, :, SCALE_ROWS * quadrant : SCALE_ROWS * (quadrant + 1), :],
                 )
 
         def load_window(b):
@@ -96,7 +96,7 @@ def tile_picked_wkvput_tanh_l_kernel(tc, x_words, x_scales, mem, w1, slot, out):
                     lhsT=w_codes[b][:].bitcast(FP8X4),
                     lhsT_scale=w_scale[b][:],
                     rhs=x_codes[piece][:, token - first : token - first + width].bitcast(FP8X4),
-                    rhs_scale=x_scale[SCALE_ROWS * plane :, column : column + width],
+                    rhs_scale=x_scale[plane // PLANES][SCALE_ROWS * (plane % PLANES) :, column : column + width],
                     start=True,
                     stop=True,
                 )
@@ -116,11 +116,12 @@ def tile_picked_wkvput_tanh_l_kernel(tc, x_words, x_scales, mem, w1, slot, out):
             nc.sync.dma_start(out=out[b * P : (b + 1) * P, :], in_=window[b][:])
 
         nc.sync.dma_start(out=w_raw[:], in_=w_rows)
-        load_scales(nc.sync, range(1))
-        load_scales(nc.scalar, range(1, QUADRANTS))
+        load_scales(nc.sync, 0, range(1))
+        load_scales(nc.scalar, 0, range(1, QUADRANTS))
         nc.sync.dma_start(offsets[:], slot)
         load_tokens(0)
         load_window(0)
+        load_scales(nc.sync, 1, range(QUADRANTS))
         load_tokens(1)
         load_window(1)
 

@@ -25,7 +25,6 @@ SCALE_ROWS = 4
 PASS = 256
 EARLY = 384
 PIECES = ((0, EARLY), (EARLY, TOKENS))
-PLANES = 2
 PSUM_BANKS = 8
 MX_ALIGN = 64
 DMA_ALIGN = 256
@@ -47,24 +46,25 @@ def tile_picked_wkvput_tanh_l_kernel(tc, x_words, x_scales, mem, w1, slot, out):
         w_codes = [keep.tile([P, P], U32, name="w_codes%d" % b, align_bytes=MX_ALIGN) for b in blocks]
         w_scale = [keep.tile([P, P], U8, name="w_scale%d" % b, align_bytes=MX_ALIGN) for b in blocks]
         x_codes = [keep.tile([P, hi - lo], U32, name="x_codes%d" % lo, align_bytes=DMA_ALIGN) for lo, hi in PIECES]
-        x_scale = [keep.tile([P, PASS], U8, name="x_scale%d" % h, align_bytes=DMA_ALIGN) for h in range(2)]
+        x_scale = [keep.tile([P, hi - lo], U8, name="x_scale%d" % lo, align_bytes=DMA_ALIGN) for lo, hi in PIECES]
         window = [keep.tile([P, SLOTS], F32, name="window%d" % b, align_bytes=DMA_ALIGN) for b in blocks]
         y = [keep.tile([P, TOKENS], F32, name="y%d" % b) for b in blocks]
 
         w_rows = w1.rearrange("(p t) n -> p t n", t=PACK)
         x_word_view = x_words[0].rearrange("p n t -> p (n t)").bitcast(I32)
-        x_scale_view = x_scales[0].bitcast(I32).rearrange("q (h a n) -> h a q n", h=2, a=PLANES)
+        x_scale_view = x_scales[0].bitcast(I32)
 
         def load_tokens(piece):
             lo, hi = PIECES[piece]
             nc.sync.dma_start(out=x_codes[piece][:].bitcast(I32), in_=x_word_view[:, lo:hi])
 
-        def load_scales(queue, half, quadrants):
+        def load_scales(queue, piece, quadrants):
+            lo, hi = PIECES[piece]
             for quadrant in quadrants:
-                first = QUADRANT * quadrant
+                first = QUADRANT * quadrant + SCALE_ROWS * piece
                 queue.dma_start(
-                    out=x_scale[half][first : first + PLANES * SCALE_ROWS, :].bitcast(I32),
-                    in_=x_scale_view[half, :, SCALE_ROWS * quadrant : SCALE_ROWS * (quadrant + 1), :],
+                    out=x_scale[piece][first : first + SCALE_ROWS, :].bitcast(I32),
+                    in_=x_scale_view[SCALE_ROWS * quadrant : SCALE_ROWS * (quadrant + 1), lo // PACK : hi // PACK],
                 )
 
         def load_window(b):
@@ -88,15 +88,14 @@ def tile_picked_wkvput_tanh_l_kernel(tc, x_words, x_scales, mem, w1, slot, out):
             first = PIECES[piece][0]
             token = lo
             while token < hi:
-                plane, column = divmod(token, PASS)
-                width = min(widest, PASS - column, hi - token)
+                width = min(widest, hi - token)
                 acc = psum.tile([P, width], F32, name="acc", bufs=PSUM_BANKS)
                 nc.tensor.matmul_mx(
                     out=acc[:],
                     lhsT=w_codes[b][:].bitcast(FP8X4),
                     lhsT_scale=w_scale[b][:],
                     rhs=x_codes[piece][:, token - first : token - first + width].bitcast(FP8X4),
-                    rhs_scale=x_scale[plane // PLANES][SCALE_ROWS * (plane % PLANES) :, column : column + width],
+                    rhs_scale=x_scale[piece][SCALE_ROWS * piece :, token - first : token - first + width],
                     start=True,
                     stop=True,
                 )
@@ -133,8 +132,9 @@ def tile_picked_wkvput_tanh_l_kernel(tc, x_words, x_scales, mem, w1, slot, out):
         quantise_weights(1)
         vector_scatter(0, 0, EARLY)
         project(1, 0, EARLY, PASS)
-        project(1, EARLY, TOKENS, PASS)
-        project(0, EARLY, TOKENS, PASS)
+        for b in (1, 0):
+            project(b, EARLY, EARLY + SHORT_PASS, SHORT_PASS)
+            project(b, EARLY + SHORT_PASS, TOKENS, PASS)
         vector_scatter(1, 0, TOKENS)
         scalar_scatter(0, EARLY, SCALAR_CUT)
         scalar_scatter(0, SCALAR_CUT, TOKENS)

@@ -23,14 +23,15 @@ QUADRANT = 32
 QUADRANTS = P // QUADRANT
 SCALE_ROWS = 4
 PASS = 256
+SHORT_PASS = 128
 EARLY = 384
-PIECES = ((0, EARLY), (EARLY, TOKENS))
-PSUM_BANKS = 8
+SCALE_CUT = 640
+PIECES = ((0, EARLY), (EARLY, SCALE_CUT), (SCALE_CUT, TOKENS))
 MX_ALIGN = 64
 DMA_ALIGN = 256
 VECTOR_COLUMNS = 64
-SHORT_PASS = 128
 SCALAR_CUT = 768
+WINDOW_CUT = 1536
 
 
 def tile_picked_wkvput_tanh_l_kernel(tc, x_words, x_scales, mem, w1, slot, out):
@@ -46,9 +47,10 @@ def tile_picked_wkvput_tanh_l_kernel(tc, x_words, x_scales, mem, w1, slot, out):
         w_codes = [keep.tile([P, P], U32, name="w_codes%d" % b, align_bytes=MX_ALIGN) for b in blocks]
         w_scale = [keep.tile([P, P], U8, name="w_scale%d" % b, align_bytes=MX_ALIGN) for b in blocks]
         x_codes = [keep.tile([P, hi - lo], U32, name="x_codes%d" % lo, align_bytes=DMA_ALIGN) for lo, hi in PIECES]
-        x_scale = [keep.tile([P, hi - lo], U8, name="x_scale%d" % lo, align_bytes=DMA_ALIGN) for lo, hi in PIECES]
+        x_scale = keep.tile([P, TOKENS], U8, name="x_scale", align_bytes=DMA_ALIGN)
         window = [keep.tile([P, SLOTS], F32, name="window%d" % b, align_bytes=DMA_ALIGN) for b in blocks]
         y = [keep.tile([P, TOKENS], F32, name="y%d" % b) for b in blocks]
+        staged = keep.tile([P, SHORT_PASS], F32, name="staged")
 
         w_rows = w1.rearrange("(p t) n -> p t n", t=PACK)
         x_word_view = x_words[0].rearrange("p n t -> p (n t)").bitcast(I32)
@@ -58,17 +60,16 @@ def tile_picked_wkvput_tanh_l_kernel(tc, x_words, x_scales, mem, w1, slot, out):
             lo, hi = PIECES[piece]
             nc.sync.dma_start(out=x_codes[piece][:].bitcast(I32), in_=x_word_view[:, lo:hi])
 
-        def load_scales(queue, piece, quadrants):
-            lo, hi = PIECES[piece]
+        def load_scales(queue, quadrants, lo, hi):
             for quadrant in quadrants:
-                first = QUADRANT * quadrant + SCALE_ROWS * piece
+                first = QUADRANT * quadrant
                 queue.dma_start(
-                    out=x_scale[piece][first : first + SCALE_ROWS, :].bitcast(I32),
+                    out=x_scale[first : first + SCALE_ROWS, lo:hi].bitcast(I32),
                     in_=x_scale_view[SCALE_ROWS * quadrant : SCALE_ROWS * (quadrant + 1), lo // PACK : hi // PACK],
                 )
 
-        def load_window(b):
-            nc.sync.dma_start(out=window[b][:], in_=mem[b * P : (b + 1) * P, :])
+        def load_window(b, lo, hi):
+            nc.sync.dma_start(out=window[b][:, lo:hi], in_=mem[b * P : (b + 1) * P, lo:hi])
 
         def round_weights(copy, b, lo, hi):
             copy(
@@ -83,24 +84,27 @@ def tile_picked_wkvput_tanh_l_kernel(tc, x_words, x_scales, mem, w1, slot, out):
                 in_=w_bf16[b][:].rearrange("p n t -> p (n t)"),
             )
 
-        def project(b, lo, hi, widest):
-            piece = 0 if lo < EARLY else 1
+        def project(b, lo, hi, bank, result):
+            piece = max(i for i in range(len(PIECES)) if PIECES[i][0] <= lo)
             first = PIECES[piece][0]
-            token = lo
-            while token < hi:
-                width = min(widest, hi - token)
-                acc = psum.tile([P, width], F32, name="acc", bufs=PSUM_BANKS)
-                nc.tensor.matmul_mx(
-                    out=acc[:],
-                    lhsT=w_codes[b][:].bitcast(FP8X4),
-                    lhsT_scale=w_scale[b][:],
-                    rhs=x_codes[piece][:, token - first : token - first + width].bitcast(FP8X4),
-                    rhs_scale=x_scale[piece][SCALE_ROWS * piece :, token - first : token - first + width],
-                    start=True,
-                    stop=True,
-                )
-                nc.scalar.activation(out=y[b][:, token : token + width], in_=acc[:], func=TANH)
-                token = token + width
+            acc = psum.tile([P, hi - lo], F32, name="acc%d" % bank)
+            nc.tensor.matmul_mx(
+                out=acc[:],
+                lhsT=w_codes[b][:].bitcast(FP8X4),
+                lhsT_scale=w_scale[b][:],
+                rhs=x_codes[piece][:, lo - first : hi - first].bitcast(FP8X4),
+                rhs_scale=x_scale[:, lo:hi],
+                start=True,
+                stop=True,
+            )
+            nc.scalar.activation(out=result, in_=acc[:], func=TANH)
+
+        def direct(b, lo, hi, bank):
+            project(b, lo, hi, bank, y[b][:, lo:hi])
+
+        def relayed(b, lo, hi, bank):
+            project(b, lo, hi, bank, staged[:])
+            nc.vector.tensor_copy(y[b][:, lo:hi], staged[:])
 
         def target(b, lo, hi):
             return window[b][:].indirect(offsets[:, lo // GROUP : hi // GROUP])
@@ -115,26 +119,36 @@ def tile_picked_wkvput_tanh_l_kernel(tc, x_words, x_scales, mem, w1, slot, out):
             nc.sync.dma_start(out=out[b * P : (b + 1) * P, :], in_=window[b][:])
 
         nc.sync.dma_start(out=w_raw[:], in_=w_rows)
-        load_scales(nc.sync, 0, range(1))
-        load_scales(nc.scalar, 0, range(1, QUADRANTS))
+        load_scales(nc.sync, range(1), 0, TOKENS)
+        load_scales(nc.scalar, range(1, 2), 0, TOKENS)
+        load_scales(nc.scalar, range(2, QUADRANTS), 0, SCALE_CUT)
         nc.sync.dma_start(offsets[:], slot)
         load_tokens(0)
-        load_window(0)
-        load_scales(nc.sync, 1, range(QUADRANTS))
+        load_window(0, 0, WINDOW_CUT)
+        load_window(0, WINDOW_CUT, SLOTS)
         load_tokens(1)
-        load_window(1)
+        load_scales(nc.sync, range(2, QUADRANTS), SCALE_CUT, TOKENS)
+        load_tokens(2)
+        load_window(1, 0, SLOTS)
 
         round_weights(nc.vector.tensor_copy, 0, 0, VECTOR_COLUMNS)
         round_weights(nc.scalar.copy, 0, VECTOR_COLUMNS, P)
         quantise_weights(0)
         round_weights(nc.scalar.copy, 1, 0, P)
-        project(0, 0, EARLY, SHORT_PASS)
+        direct(0, 0, 128, 0)
+        direct(0, 128, 256, 1)
+        direct(0, 256, 384, 2)
         quantise_weights(1)
+        relayed(1, 0, 128, 3)
         vector_scatter(0, 0, EARLY)
-        project(1, 0, EARLY, PASS)
-        for b in (1, 0):
-            project(b, EARLY, EARLY + SHORT_PASS, SHORT_PASS)
-            project(b, EARLY + SHORT_PASS, TOKENS, PASS)
+        direct(1, 128, 384, 4)
+        direct(0, 384, 640, 5)
+        direct(1, 384, 640, 7)
+        direct(0, 640, 768, 6)
+        direct(1, 640, 896, 0)
+        direct(1, 896, 1024, 1)
+        relayed(0, 896, 1024, 2)
+        direct(0, 768, 896, 6)
         vector_scatter(1, 0, TOKENS)
         scalar_scatter(0, EARLY, SCALAR_CUT)
         scalar_scatter(0, SCALAR_CUT, TOKENS)

from contextlib import ExitStack

import concourse.mybir as mybir

F32 = mybir.dt.float32
BF16 = mybir.dt.bfloat16
I32 = mybir.dt.int32
U32 = mybir.dt.uint32
U16 = mybir.dt.uint16
U8 = mybir.dt.uint8
FP8X4 = mybir.dt.float8_e4m3fn_x4
TANH = mybir.ActivationFunctionType.Tanh
COPY = mybir.ActivationFunctionType.Copy

K, TOKENS, ROWS, SLOTS = 512, 1024, 256, 2048
FLOPS = 2 * K * TOKENS * ROWS

P = 128
BLOCKS = ROWS // P
PACK = 4
GROUP = 16
QUADRANT = 32
QUADRANTS = P // QUADRANT
SCALE_ROWS = 4
PASS = 256
SHORT_PASS = 128
EARLY = 384
SCALE_CUT = 640
PIECES = ((0, EARLY), (EARLY, SCALE_CUT), (SCALE_CUT, TOKENS))
MX_ALIGN = 64
DMA_ALIGN = 256
VECTOR_COLUMNS = 64
SCALAR_CUT = 768
WINDOW_CUT = 1536


def tile_picked_wkvput_tanh_l_kernel(tc, x_words, x_scales, mem, w1, slot, out):
    nc = tc.nc
    with ExitStack() as ctx:
        keep = ctx.enter_context(tc.tile_pool(name="keep", bufs=1))
        psum = ctx.enter_context(tc.psum_pool(name="psum", bufs=1))

        blocks = range(BLOCKS)
        offsets = keep.tile([P, TOKENS // GROUP], U16, name="offsets", align_bytes=DMA_ALIGN)
        w_raw = keep.tile([P, PACK, ROWS], F32, name="w_raw", align_bytes=DMA_ALIGN)
        w_bf16 = [keep.tile([P, P, PACK], BF16, name="w_bf16_%d" % b, align_bytes=MX_ALIGN) for b in blocks]
        w_codes = [keep.tile([P, P], U32, name="w_codes%d" % b, align_bytes=MX_ALIGN) for b in blocks]
        w_scale = [keep.tile([P, P], U8, name="w_scale%d" % b, align_bytes=MX_ALIGN) for b in blocks]
        x_codes = [keep.tile([P, hi - lo], U32, name="x_codes%d" % lo, align_bytes=DMA_ALIGN) for lo, hi in PIECES]
        x_scale = keep.tile([P, TOKENS], U8, name="x_scale", align_bytes=DMA_ALIGN)
        window = [keep.tile([P, SLOTS], F32, name="window%d" % b, align_bytes=DMA_ALIGN) for b in blocks]
        y = [keep.tile([P, TOKENS], F32, name="y%d" % b) for b in blocks]
        staged = keep.tile([P, SHORT_PASS], F32, name="staged")

        w_rows = w1.rearrange("(p t) n -> p t n", t=PACK)
        x_word_view = x_words[0].rearrange("p n t -> p (n t)").bitcast(I32)
        x_scale_view = x_scales[0].bitcast(I32)

        def load_tokens(piece):
            lo, hi = PIECES[piece]
            nc.sync.dma_start(out=x_codes[piece][:].bitcast(I32), in_=x_word_view[:, lo:hi])

        def load_scales(queue, quadrants, lo, hi):
            for quadrant in quadrants:
                first = QUADRANT * quadrant
                queue.dma_start(
                    out=x_scale[first : first + SCALE_ROWS, lo:hi].bitcast(I32),
                    in_=x_scale_view[SCALE_ROWS * quadrant : SCALE_ROWS * (quadrant + 1), lo // PACK : hi // PACK],
                )

        def load_window(b, lo, hi):
            nc.sync.dma_start(out=window[b][:, lo:hi], in_=mem[b * P : (b + 1) * P, lo:hi])

        def round_weights(copy, b, lo, hi):
            copy(
                out=w_bf16[b][:, lo:hi, :].rearrange("p (c i) t -> p c t i", i=PACK),
                in_=w_raw[:, :, b * P + lo : b * P + hi].rearrange("p t (c i) -> p c t i", i=PACK),
            )

        def quantise_weights(b):
            nc.vector.quantize_mx(
                out=w_codes[b][:].bitcast(FP8X4),
                scales=w_scale[b][:],
                in_=w_bf16[b][:].rearrange("p n t -> p (n t)"),
            )

        def project(b, lo, hi, bank, result):
            piece = max(i for i in range(len(PIECES)) if PIECES[i][0] <= lo)
            first = PIECES[piece][0]
            acc = psum.tile([P, hi - lo], F32, name="acc%d" % bank)
            nc.tensor.matmul_mx(
                out=acc[:],
                lhsT=w_codes[b][:].bitcast(FP8X4),
                lhsT_scale=w_scale[b][:],
                rhs=x_codes[piece][:, lo - first : hi - first].bitcast(FP8X4),
                rhs_scale=x_scale[:, lo:hi],
                start=True,
                stop=True,
            )
            nc.scalar.activation(out=result, in_=acc[:], func=TANH)

        def direct(b, lo, hi, bank):
            project(b, lo, hi, bank, y[b][:, lo:hi])

        def relayed(b, lo, hi, bank):
            project(b, lo, hi, bank, staged[:])
            nc.vector.tensor_copy(y[b][:, lo:hi], staged[:])

        def target(b, lo, hi):
            return window[b][:].indirect(offsets[:, lo // GROUP : hi // GROUP])

        def vector_scatter(b, lo, hi):
            nc.vector.tensor_copy(target(b, lo, hi), y[b][:, lo:hi])

        def scalar_scatter(b, lo, hi):
            nc.scalar.activation(out=target(b, lo, hi), in_=y[b][:, lo:hi], func=COPY)

        def store_window(b):
            nc.sync.dma_start(out=out[b * P : (b + 1) * P, :], in_=window[b][:])

        nc.sync.dma_start(out=w_raw[:], in_=w_rows)
        load_scales(nc.sync, range(1), 0, TOKENS)
        load_scales(nc.scalar, range(1, 2), 0, TOKENS)
        load_scales(nc.scalar, range(2, QUADRANTS), 0, SCALE_CUT)
        nc.sync.dma_start(offsets[:], slot)
        load_tokens(0)
        load_window(0, 0, WINDOW_CUT)
        load_window(0, WINDOW_CUT, SLOTS)
        load_tokens(1)
        load_scales(nc.sync, range(2, QUADRANTS), SCALE_CUT, TOKENS)
        load_tokens(2)
        load_window(1, 0, SLOTS)

        round_weights(nc.vector.tensor_copy, 0, 0, VECTOR_COLUMNS)
        round_weights(nc.scalar.copy, 0, VECTOR_COLUMNS, P)
        quantise_weights(0)
        round_weights(nc.scalar.copy, 1, 0, P)
        direct(0, 0, 128, 0)
        direct(0, 128, 256, 1)
        direct(0, 256, 384, 2)
        quantise_weights(1)
        relayed(1, 0, 128, 3)
        vector_scatter(0, 0, EARLY)
        direct(1, 128, 384, 4)
        direct(0, 384, 640, 5)
        direct(1, 384, 640, 7)
        direct(0, 640, 768, 6)
        direct(1, 640, 896, 0)
        direct(1, 896, 1024, 1)
        relayed(0, 896, 1024, 2)
        direct(0, 768, 896, 6)
        vector_scatter(1, 0, TOKENS)
        scalar_scatter(0, EARLY, SCALAR_CUT)
        scalar_scatter(0, SCALAR_CUT, TOKENS)
        store_window(0)
        store_window(1)
